import numpy as np
import ml_dtypes


def mxq(x, axis, fmt="e4m3"):
    dtype, down = {"e4m3": (ml_dtypes.float8_e4m3fn, 7), "e5m2": (ml_dtypes.float8_e5m2, 14)}[fmt]
    v = np.moveaxis(np.asarray(x, np.float32).astype(ml_dtypes.bfloat16).astype(np.float64), axis, -1)
    blocks = v.reshape(v.shape[:-1] + (-1, 32))
    amax = np.abs(blocks).max(-1, keepdims=True)
    byte = np.maximum(np.where(amax > 0, np.frexp(amax)[1] - 1 + 127, 0) - down, 1)
    scale = np.exp2(byte - 127.0)
    codes = (blocks / scale).astype(np.float32).astype(dtype).astype(np.float64)
    return np.moveaxis((codes * scale).reshape(v.shape), -1, axis)


WIDE = False


def mx_kscale(k):
    if not WIDE:
        return np.ones(k)
    levels = np.array([10, -10, 5, -5, 0])
    if k % 512:
        return np.exp2(np.random.permutation(np.resize(levels, k // 32))).repeat(32)
    a = np.empty((k // 512, 16))
    for p in range(k // 512):
        a[p, :8] = np.random.permutation(np.resize(levels, 8))
        for g in range(8):
            far = levels[np.abs(levels - a[p, g]) >= 10]
            a[p, g + 8] = far[np.random.randint(len(far))]
    return np.exp2(a.ravel()).repeat(32)


def f64(x):
    return np.asarray(x).astype(np.float64)


def striped(idx):
    return np.tile(idx.reshape(-1, 16).T, (8, 1)).astype(np.uint16)


def unstriped(offs):
    return offs[:16].T.reshape(-1).astype(np.int64)


E2M1 = np.array([0.0, 0.5, 1.0, 1.5, 2.0, 3.0, 4.0, 6.0, -0.0, -0.5, -1.0, -1.5, -2.0, -3.0, -4.0, -6.0])


def pack_weight(w, fmt):
    k, n = w.shape
    w = f64(np.asarray(w, np.float32).astype(ml_dtypes.bfloat16)).reshape(k // 32, 32, n)
    amax = np.abs(w).max(1)
    if fmt == "e4m3":
        byte = np.frexp(amax)[1] - 1 + 127 - 7
    else:
        mant, ex = np.frexp(amax / 6.0)
        byte = np.where(mant > 0.5, ex, ex - 1) + 127
    byte = np.clip(np.where(amax > 0, byte, 1), 1, 254)
    scaled = (w * np.exp2(127.0 - byte)[:, None, :]).reshape(k, n).astype(np.float32)
    by_word = np.ascontiguousarray(scaled.reshape(k // 512, 128, 4, n).transpose(0, 1, 3, 2))
    if fmt == "e4m3":
        words = by_word.astype(ml_dtypes.float8_e4m3fn).view(np.uint8)
    else:
        c = by_word.astype(ml_dtypes.float4_e2m1fn).view(np.uint8) & 0xF
        words = (c[..., 0::2] | (c[..., 1::2] << 4)).reshape(k // 512, 128, 2 * n)
    return np.ascontiguousarray(words), np.ascontiguousarray(byte.astype(np.uint8).reshape(k // 512, 16, n))


def unpack_weight(words, scales, fmt):
    g, _, n = scales.shape
    words = np.ascontiguousarray(words).reshape(g, 128, n, -1)
    if fmt == "e4m3":
        vals = words.view(ml_dtypes.float8_e4m3fn).astype(np.float64)
    else:
        nib = np.empty((g, 128, n, 4), np.uint8)
        nib[..., 0::2] = words & 0xF
        nib[..., 1::2] = words >> 4
        vals = E2M1[nib]
    vals = vals * np.repeat(np.exp2(scales.astype(np.float64) - 127.0), 8, axis=1)[..., None]
    return vals.transpose(0, 1, 3, 2).reshape(g * 512, n)


def gelu(v):
    return 0.5 * v * (1.0 + np.tanh(np.sqrt(2.0 / np.pi) * (v + 0.044715 * v**3)))


def striped8(idx):
    return np.concatenate([v.reshape(-1, 16).T for v in idx]).astype(np.uint16)


def unstriped8(offs):
    return np.stack([offs[16 * g:16 * g + 16].T.reshape(-1) for g in range(8)]).astype(np.int64)


def heads(h, wgt, idx8):
    r = np.arange(h.shape[0])
    return wgt[r // 4 % 128] * h[r[:, None], idx8[r % 512 // 64]]


K, T, S, H, T2, P, N = 1536, 2048, 512, 1024, 1024, 512, 768

def setup_inputs():
    n = np.random.standard_normal
    s = mx_kscale(K)[:, None]
    u = mx_kscale(H)[:, None]
    tab_words, tab_scales = pack_weight(n((K, T)) * s, "e4m3")
    w4_words, w4_scales = pack_weight(n((H, N)) / np.sqrt(H) / u, "e2m1")
    idx8 = np.stack([np.random.permutation(T2)[:P] for _ in range(8)])
    return {
        "tab_words": tab_words, "tab_scales": tab_scales,
        "offs": striped(np.random.permutation(T)[:S]),
        "offs2": striped(np.random.permutation(T2)[:S]),
        "offs3": striped8(idx8),
        "w1": (1.5 * n((K, H)) / np.sqrt(K) / s).astype(np.float32),
        "gain": (np.random.uniform(0.8, 2.2, H) * u[:, 0]).astype(np.float32),
        "res": (0.7 * n((H, S)) * u).astype(np.float32),
        "wgs": np.exp(0.3 * n((128, S))).astype(np.float32),
        "page0": (n((H, T2)) * u).astype(np.float32),
        "wgt": np.repeat(np.random.uniform(0.5, 2.0, (8, P)), 16, axis=0).astype(np.float32),
        "thr": (0.7 * n(H) * u[:, 0]).astype(np.float32),
        "w4_words": w4_words, "w4_scales": w4_scales,
        "base": (0.7 * n((N, P))).astype(np.float32),
    }

def reference(tab_words, tab_scales, offs, offs2, offs3, w1, gain, res, wgs, page0, wgt, thr, w4_words, w4_scales, base):
    v = unpack_weight(tab_words, tab_scales, "e4m3")[:, unstriped(offs)]
    w4 = unpack_weight(w4_words, w4_scales, "e2m1")
    w1q = mxq(f64(w1), 0, "e4m3")
    h = f64(gain)[:, None] * np.tanh(w1q.T @ v) + f64(res)
    page = f64(page0).copy()
    page[:, unstriped(offs2)] = np.tile(f64(wgs), (H // 128, 1)) * h
    x = heads(page, f64(wgt), unstriped8(offs3))
    z = np.maximum(x, f64(thr)[:, None])
    zq = mxq(z, 0, "e4m3")
    return (w4.T @ zq) + f64(base)

@@ -1,0 +1,264 @@
+from contextlib import ExitStack
+
+import concourse.mybir as mybir
+from concourse.masks import make_identity
+
+K, T, S, H, T2, M, N = 1536, 2048, 512, 1024, 1024, 512, 768
+FLOPS = 2 * K * H * S + 2 * H * N * M
+
+F32 = mybir.dt.float32
+BF16 = mybir.dt.bfloat16
+I32 = mybir.dt.int32
+U32 = mybir.dt.uint32
+U16 = mybir.dt.uint16
+U8 = mybir.dt.uint8
+FP8X4 = mybir.dt.float8_e4m3fn_x4
+FP4X4 = mybir.dt.float4_e2m1fn_x4
+ALU = mybir.AluOpType
+ACT = mybir.ActivationFunctionType
+
+P = 128
+PACK = 4
+PASS = P * PACK
+KP = K // PASS
+HB = H // PASS
+NT = N // P
+HALF = M // 2
+
+
+def tile_list_cable_tension_display_kernel(
+    tc, tab_words, tab_scales, offs, offs2, offs3, w1, gain, res, wgs, page0, wgt, thr, w4_words, w4_scales, base, out
+):
+    nc = tc.nc
+    with ExitStack() as ctx:
+        keep = ctx.enter_context(tc.tile_pool(name="keep", bufs=1))
+        ring = ctx.enter_context(tc.tile_pool(name="ring", bufs=3))
+        psum = ctx.enter_context(tc.psum_pool(name="psum", bufs=1))
+
+        def kept(shape, dtype, name):
+            return keep.tile(shape, dtype, name=name, align_bytes=64)
+
+        list1 = kept([P, S // 16], U16, "list1")
+        list2 = kept([P, S // 16], U16, "list2")
+        list3 = kept([P, M // 16], U16, "list3")
+        tabw = [kept([P, T], I32, f"tabw{a}") for a in range(KP)]
+        tabs = kept([P, T], U8, "tabs")
+        vw = [kept([P, S], U32, f"vw{a}") for a in range(KP)]
+        vs = kept([P, S], U8, "vs")
+        w1raw = [[kept([P, PACK, PASS], F32, f"w1raw{b}{a}") for a in range(KP)] for b in range(HB)]
+        w1c = [[kept([P, PASS], U32, f"w1c{b}{a}") for a in range(KP)] for b in range(HB)]
+        w1s = [[kept([P, PASS], U8, f"w1s{b}{a}") for a in range(KP)] for b in range(HB)]
+        page = [[kept([P, T2], F32, f"page{b}{i}") for i in range(PACK)] for b in range(HB)]
+        h0 = [kept([P, S], F32, f"h0{i}") for i in range(PACK)]
+        h1 = kept([P, PACK, S], F32, "h1")
+        hres = [[t[:] for t in h0], [h1[:, i, :] for i in range(PACK)]]
+        wgsd = [kept([P, S], F32, f"wgsd{i}") for i in range(PACK)]
+        wgt_t = kept([P, M], F32, "wgt_t")
+        gain_t = kept([P, HB, PACK], F32, "gain_t")
+        thr_t = kept([P, HB, PACK], F32, "thr_t")
+        w4w = kept([P, HB, 2 * N], U8, "w4w")
+        w4s = kept([P, HB, N], U8, "w4s")
+        x = kept([P, PACK, M], F32, "x")
+        zplanes = kept([P, PACK, M], BF16, "zplanes")
+        z0 = kept([P, M * PACK], BF16, "z0")
+        z0c = kept([P, M], U32, "z0c")
+        z0s = kept([P, M], U8, "z0s")
+        z1 = [kept([P, HALF * PACK], BF16, f"z1{hf}") for hf in range(2)]
+        z1c = [kept([P, HALF], U32, f"z1c{hf}") for hf in range(2)]
+        z1s = [kept([P, HALF], U8, f"z1s{hf}") for hf in range(2)]
+        acc = [[kept([P, 2, HALF], F32, f"acc{hf}{q}") for q in range(NT // 2)] for hf in range(2)]
+        ident = kept([P, P], F32, "ident")
+
+        def bank(number, shape):
+            return psum.tile(shape, F32, name=f"bank{number}")
+
+        res_v = res.rearrange("(b p i) j -> b i p j", b=HB, i=PACK)
+        page_v = page0.rearrange("(b p i) c -> b i p c", b=HB, i=PACK)
+        wgs_v = wgs.rearrange("(q i) j -> i q j", i=PACK)
+        base_v = base.rearrange("(q u p) m -> q p u m", u=2, p=P)
+        out_v = out.rearrange("(q u p) m -> q p u m", u=2, p=P)
+
+        def load_w1(b, a):
+            rows = w1[a * PASS : (a + 1) * PASS, b * PASS : (b + 1) * PASS]
+            nc.sync.dma_start(out=w1raw[b][a][:], in_=rows.rearrange("(p j) c -> p j c", j=PACK))
+
+        def load_tab(a):
+            nc.sync.dma_start(out=tabw[a][:], in_=tab_words[a].rearrange("p n t -> p (n t)").bitcast(I32))
+
+        def load_wgs(i):
+            for quad in range(4):
+                nc.sync.dma_start(out=wgsd[i][32 * quad : 32 * (quad + 1), :], in_=wgs_v[i])
+
+        def load_res(b, i):
+            nc.sync.dma_start(out=hres[b][i], in_=res_v[b, i])
+
+        def load_page(b, i):
+            nc.sync.dma_start(out=page[b][i][:], in_=page_v[b, i])
+
+        nc.vector.memset(tabs[:].bitcast(I32), 0)
+        for quad in range(4):
+            nc.scalar.dma_start(
+                out=tabs[32 * quad : 32 * quad + PACK * KP, :].bitcast(I32),
+                in_=tab_scales[:, PACK * quad : PACK * (quad + 1), :].bitcast(I32),
+            )
+
+        nc.gpsimd.memset(w4s[:].bitcast(I32), 0)
+        make_identity(nc, ident[:])
+
+        nc.sync.dma_start(list1[:], offs)
+        load_w1(0, 0)
+        load_tab(0)
+        nc.sync.dma_start(out=gain_t[:], in_=gain.rearrange("(b p i) -> p b i", b=HB, i=PACK))
+        nc.sync.dma_start(list2[:], offs2)
+        load_w1(0, 1)
+        load_tab(1)
+        load_w1(0, 2)
+        load_tab(2)
+        load_res(0, 0)
+        load_wgs(0)
+        load_page(0, 0)
+        for i in range(1, PACK):
+            load_res(0, i)
+        load_wgs(1)
+        load_page(0, 1)
+        load_w1(1, 0)
+        load_wgs(2)
+        load_page(0, 2)
+        load_w1(1, 1)
+        load_wgs(3)
+        load_page(0, 3)
+        load_w1(1, 2)
+        nc.sync.dma_start(out=h1[:], in_=res[PASS:, :].rearrange("(p i) j -> p i j", i=PACK))
+        nc.sync.dma_start(list3[:], offs3)
+        nc.sync.dma_start(out=thr_t[:], in_=thr.rearrange("(b p i) -> p b i", b=HB, i=PACK))
+        load_page(1, 0)
+        nc.sync.dma_start(out=wgt_t[:], in_=wgt)
+        for i in range(1, PACK):
+            load_page(1, i)
+        for quad in range(4):
+            nc.sync.dma_start(
+                out=w4s[32 * quad : 32 * quad + PACK, :, :].bitcast(I32),
+                in_=w4_scales[:, PACK * quad : PACK * (quad + 1), :].rearrange("a r n -> r a n").bitcast(I32),
+            )
+        nc.sync.dma_start(out=w4w[:].bitcast(I32), in_=w4_words.rearrange("a p n -> p a n").bitcast(I32))
+        for hf in range(2):
+            for q in range(NT // 2):
+                nc.sync.dma_start(out=acc[hf][q][:], in_=base_v[q, :, :, hf * HALF : (hf + 1) * HALF])
+
+        def quantise_w1(b, a, on_vector):
+            grouped = ring.tile([P, PASS * PACK], BF16, name="grouped", align_bytes=64)
+            dst = grouped[:].rearrange("p (t m j) -> p m j t", t=PACK, j=PACK)
+            src = w1raw[b][a][:].rearrange("p j (m t) -> p m j t", t=PACK)
+            if on_vector:
+                nc.vector.tensor_copy(out=dst, in_=src)
+            else:
+                nc.scalar.copy(out=dst, in_=src)
+            nc.vector.quantize_mx(out=w1c[b][a][:].bitcast(FP8X4), scales=w1s[b][a][:], in_=grouped[:])
+
+        def features(b, i, on_vector):
+            y = bank(i % 2, [P, S])
+            cols = slice(i * P, (i + 1) * P)
+            for a in range(KP):
+                nc.tensor.matmul_mx(
+                    out=y[:],
+                    lhsT=w1c[b][a][:, cols].bitcast(FP8X4),
+                    lhsT_scale=w1s[b][a][:, cols],
+                    rhs=vw[a][:].bitcast(FP8X4),
+                    rhs_scale=vs[PACK * a : P, :],
+                    start=(a == 0),
+                    stop=(a == KP - 1),
+                )
+            bounded = ring.tile([P, S], F32, name="bounded", bufs=4)
+            nc.scalar.activation(out=bounded[:], in_=y[:], func=ACT.Tanh)
+            factor = gain_t[:, b, i : i + 1]
+            if on_vector:
+                nc.vector.scalar_tensor_tensor(
+                    out=hres[b][i], in0=bounded[:], scalar=factor, in1=hres[b][i], op0=ALU.mult, op1=ALU.add
+                )
+                return
+            scaled = ring.tile([P, S], F32, name="scaled", bufs=2)
+            nc.scalar.activation(out=scaled[:], in_=bounded[:], func=ACT.Copy, scale=factor)
+            turned = bank(2 + i % 2, [P, S])
+            for c in range(S // P):
+                block = slice(c * P, (c + 1) * P)
+                nc.tensor.matmul(turned[:, block], hres[b][i][:, block], ident[:], start=True, stop=False, is_transpose=True)
+                nc.tensor.matmul(turned[:, block], scaled[:, block], ident[:], start=False, stop=True, is_transpose=True)
+            summed = ring.tile([P, S], F32, name="summed", bufs=2)
+            nc.scalar.copy(out=summed[:], in_=turned[:])
+            back = bank(4 + i % 2, [P, S])
+            for c in range(S // P):
+                block = slice(c * P, (c + 1) * P)
+                nc.tensor.transpose(back[:, block], summed[:, block], ident[:])
+            nc.scalar.copy(out=hres[b][i], in_=back[:])
+
+        def put(b, i):
+            nc.vector.tensor_tensor(page[b][i][:].indirect(list2[:]), hres[b][i], wgsd[i][:], ALU.mult)
+
+        def pick(x, b, i):
+            nc.vector.tensor_tensor(x[:, i, :], page[b][i][:].indirect(list3[:]), wgt_t[:], ALU.mult)
+
+        def display(obank, b, hf, codes, scales):
+            for q in range(NT // 2):
+                for u in range(2):
+                    n = 2 * q + u
+                    nc.tensor.matmul_mx(
+                        out=obank[hf][q][:, u, :],
+                        lhsT=w4w[:, b, 2 * P * n : 2 * P * (n + 1)].bitcast(FP4X4),
+                        lhsT_scale=w4s[:, b, P * n : P * (n + 1)],
+                        rhs=codes.bitcast(FP8X4),
+                        rhs_scale=scales,
+                        start=(b == 0 and u == 0),
+                        stop=(b == HB - 1 and u == 1),
+                    )
+
+        nc.vector.tensor_copy(vs[:], tabs[:].indirect(list1[:]))
+        for a in range(KP):
+            quantise_w1(0, a, a == KP - 1)
+            nc.vector.tensor_copy(vw[a][:], tabw[a][:].bitcast(U32).indirect(list1[:]))
+
+        features(0, 0, True)
+        put(0, 0)
+        for i in range(1, PACK):
+            features(0, i, i == 1)
+        put(0, 1)
+        quantise_w1(1, 0, False)
+        put(0, 2)
+        quantise_w1(1, 1, False)
+        put(0, 3)
+        quantise_w1(1, 2, False)
+        for i in range(PACK):
+            pick(x, 0, i)
+        for i in range(PACK):
+            nc.vector.tensor_scalar(out=zplanes[:, i, :], in0=x[:, i, :], scalar1=thr_t[:, 0, i : i + 1], scalar2=None, op0=ALU.max)
+        nc.scalar.copy(
+            out=z0[:].rearrange("p (c i t) -> p c t i", i=4, t=PACK),
+            in_=zplanes[:].rearrange("p t (c i) -> p c t i", i=4),
+        )
+
+        for i in range(PACK):
+            features(1, i, False)
+        put(1, 0)
+        nc.vector.quantize_mx(out=z0c[:].bitcast(FP8X4), scales=z0s[:], in_=z0[:])
+        obank = [[bank(2 + 3 * hf + q, [P, 2, HALF]) for q in range(NT // 2)] for hf in range(2)]
+        for hf in range(2):
+            display(obank, 0, hf, z0c[:, hf * HALF : (hf + 1) * HALF], z0s[:, hf * HALF : (hf + 1) * HALF])
+        for i in range(1, PACK):
+            put(1, i)
+        x = kept([P, PACK, M], F32, "h1")
+        for i in range(PACK):
+            pick(x, 1, i)
+        floor = thr_t[:, 1, :].unsqueeze(1).unsqueeze(3).to_broadcast([P, HALF // 4, PACK, 4])
+        for hf in range(2):
+            nc.vector.tensor_tensor(
+                z1[hf][:].rearrange("p (c i t) -> p c t i", i=4, t=PACK),
+                x[:, :, hf * HALF : (hf + 1) * HALF].rearrange("p t (c i) -> p c t i", i=4),
+                floor,
+                ALU.max,
+            )
+        for hf in range(2):
+            nc.vector.quantize_mx(out=z1c[hf][:].bitcast(FP8X4), scales=z1s[hf][:], in_=z1[hf][:])
+            display(obank, 1, hf, z1c[hf][:], z1s[hf][:])
+        for hf in range(2):
+            for q in range(NT // 2):
+                nc.vector.tensor_tensor(acc[hf][q][:], obank[hf][q][:], acc[hf][q][:], ALU.add)
+                nc.sync.dma_start(out=out_v[q, :, :, hf * HALF : (hf + 1) * HALF], in_=acc[hf][q][:])

@@ -44,7 +44,6 @@ def tile_list_cable_tension_display_kernel(
         tabw = [kept([P, T], I32, f"tabw{a}") for a in range(KP)]
         tabs = kept([P, T], U8, "tabs")
         vw = [kept([P, S], U32, f"vw{a}") for a in range(KP)]
-        vs = kept([P, S], U8, "vs")
         w1raw = [[kept([P, PACK, PASS], F32, f"w1raw{b}{a}") for a in range(KP)] for b in range(HB)]
         w1c = [[kept([P, PASS], U32, f"w1c{b}{a}") for a in range(KP)] for b in range(HB)]
         w1s = [[kept([P, PASS], U8, f"w1s{b}{a}") for a in range(KP)] for b in range(HB)]
@@ -53,6 +52,8 @@ def tile_list_cable_tension_display_kernel(
         h1 = kept([P, PACK, S], F32, "h1")
         hres = [[t[:] for t in h0], [h1[:, i, :] for i in range(PACK)]]
         wgsd = [kept([P, S], F32, f"wgsd{i}") for i in range(PACK)]
+        wgs_t = kept([P, S], F32, "wgs_t")
+        wgs_turned = kept([P, S // P, PACK, P], F32, "wgs_turned")
         wgt_t = kept([P, M], F32, "wgt_t")
         gain_t = kept([P, HB, PACK], F32, "gain_t")
         thr_t = kept([P, HB, PACK], F32, "thr_t")
@@ -74,7 +75,6 @@ def tile_list_cable_tension_display_kernel(
 
         res_v = res.rearrange("(b p i) j -> b i p j", b=HB, i=PACK)
         page_v = page0.rearrange("(b p i) c -> b i p c", b=HB, i=PACK)
-        wgs_v = wgs.rearrange("(q i) j -> i q j", i=PACK)
         base_v = base.rearrange("(q u p) m -> q p u m", u=2, p=P)
         out_v = out.rearrange("(q u p) m -> q p u m", u=2, p=P)
 
@@ -85,55 +85,51 @@ def tile_list_cable_tension_display_kernel(
         def load_tab(a):
             nc.sync.dma_start(out=tabw[a][:], in_=tab_words[a].rearrange("p n t -> p (n t)").bitcast(I32))
 
-        def load_wgs(i):
-            for quad in range(4):
-                nc.sync.dma_start(out=wgsd[i][32 * quad : 32 * (quad + 1), :], in_=wgs_v[i])
-
         def load_res(b, i):
             nc.sync.dma_start(out=hres[b][i], in_=res_v[b, i])
 
         def load_page(b, i):
             nc.sync.dma_start(out=page[b][i][:], in_=page_v[b, i])
 
-        nc.vector.memset(tabs[:].bitcast(I32), 0)
+        nc.gpsimd.memset(tabs[:].bitcast(I32), 0)
+        make_identity(nc, ident[:])
         for quad in range(4):
-            nc.scalar.dma_start(
+            nc.gpsimd.dma_start(
                 out=tabs[32 * quad : 32 * quad + PACK * KP, :].bitcast(I32),
                 in_=tab_scales[:, PACK * quad : PACK * (quad + 1), :].bitcast(I32),
             )
 
         nc.gpsimd.memset(w4s[:].bitcast(I32), 0)
-        make_identity(nc, ident[:])
 
         nc.sync.dma_start(list1[:], offs)
+        nc.sync.dma_start(out=wgs_t[:], in_=wgs)
         load_w1(0, 0)
         load_tab(0)
-        nc.sync.dma_start(out=gain_t[:], in_=gain.rearrange("(b p i) -> p b i", b=HB, i=PACK))
-        nc.sync.dma_start(list2[:], offs2)
         load_w1(0, 1)
         load_tab(1)
         load_w1(0, 2)
         load_tab(2)
+        nc.sync.dma_start(out=gain_t[:], in_=gain.rearrange("(b p i) -> p b i", b=HB, i=PACK))
         load_res(0, 0)
-        load_wgs(0)
+        nc.sync.dma_start(list2[:], offs2)
         load_page(0, 0)
-        for i in range(1, PACK):
-            load_res(0, i)
-        load_wgs(1)
+        load_res(0, 1)
         load_page(0, 1)
+        load_res(0, 2)
+        load_res(0, 3)
         load_w1(1, 0)
-        load_wgs(2)
         load_page(0, 2)
         load_w1(1, 1)
-        load_wgs(3)
         load_page(0, 3)
         load_w1(1, 2)
-        nc.sync.dma_start(out=h1[:], in_=res[PASS:, :].rearrange("(p i) j -> p i j", i=PACK))
+        load_res(1, 0)
+        load_res(1, 1)
         nc.sync.dma_start(list3[:], offs3)
         nc.sync.dma_start(out=thr_t[:], in_=thr.rearrange("(b p i) -> p b i", b=HB, i=PACK))
-        load_page(1, 0)
         nc.sync.dma_start(out=wgt_t[:], in_=wgt)
-        for i in range(1, PACK):
+        load_res(1, 2)
+        load_res(1, 3)
+        for i in range(PACK):
             load_page(1, i)
         for quad in range(4):
             nc.sync.dma_start(
@@ -152,50 +148,59 @@ def tile_list_cable_tension_display_kernel(
             if on_vector:
                 nc.vector.tensor_copy(out=dst, in_=src)
             else:
-                nc.scalar.copy(out=dst, in_=src)
+                for part in range(2):
+                    cut = slice(part * P // 2, (part + 1) * P // 2)
+                    nc.scalar.copy(out=dst[:, cut], in_=src[:, cut])
             nc.vector.quantize_mx(out=w1c[b][a][:].bitcast(FP8X4), scales=w1s[b][a][:], in_=grouped[:])
 
-        def features(b, i, on_vector):
-            y = bank(i % 2, [P, S])
+        def bounded_response(b, i, number, js):
+            width = js.stop - js.start
+            y = bank(number, [P, width])
             cols = slice(i * P, (i + 1) * P)
             for a in range(KP):
                 nc.tensor.matmul_mx(
                     out=y[:],
                     lhsT=w1c[b][a][:, cols].bitcast(FP8X4),
                     lhsT_scale=w1s[b][a][:, cols],
-                    rhs=vw[a][:].bitcast(FP8X4),
-                    rhs_scale=vs[PACK * a : P, :],
+                    rhs=vw[a][:, js].bitcast(FP8X4),
+                    rhs_scale=vs[PACK * a : P, js],
                     start=(a == 0),
                     stop=(a == KP - 1),
                 )
-            bounded = ring.tile([P, S], F32, name="bounded", bufs=4)
+            bounded = ring.tile([P, width], F32, name="bounded", bufs=4)
             nc.scalar.activation(out=bounded[:], in_=y[:], func=ACT.Tanh)
-            factor = gain_t[:, b, i : i + 1]
-            if on_vector:
-                nc.vector.scalar_tensor_tensor(
-                    out=hres[b][i], in0=bounded[:], scalar=factor, in1=hres[b][i], op0=ALU.mult, op1=ALU.add
-                )
-                return
+            return bounded
+
+        def features_on_vector(b, i, number, js):
+            bounded = bounded_response(b, i, number, js)
+            nc.vector.scalar_tensor_tensor(
+                out=hres[b][i][:, js], in0=bounded[:], scalar=gain_t[:, b, i : i + 1], in1=hres[b][i][:, js], op0=ALU.mult, op1=ALU.add
+            )
+
+        def features_on_tensor(b, i, number):
+            bounded = bounded_response(b, i, number, slice(0, S))
             scaled = ring.tile([P, S], F32, name="scaled", bufs=2)
-            nc.scalar.activation(out=scaled[:], in_=bounded[:], func=ACT.Copy, scale=factor)
-            turned = bank(2 + i % 2, [P, S])
+            nc.scalar.activation(out=scaled[:], in_=bounded[:], func=ACT.Copy, scale=gain_t[:, b, i : i + 1])
+            turned = bank(4 + i % 2, [P, S])
             for c in range(S // P):
                 block = slice(c * P, (c + 1) * P)
                 nc.tensor.matmul(turned[:, block], hres[b][i][:, block], ident[:], start=True, stop=False, is_transpose=True)
                 nc.tensor.matmul(turned[:, block], scaled[:, block], ident[:], start=False, stop=True, is_transpose=True)
             summed = ring.tile([P, S], F32, name="summed", bufs=2)
             nc.scalar.copy(out=summed[:], in_=turned[:])
-            back = bank(4 + i % 2, [P, S])
+            back = bank(6 + i % 2, [P, S])
             for c in range(S // P):
                 block = slice(c * P, (c + 1) * P)
                 nc.tensor.transpose(back[:, block], summed[:, block], ident[:])
             nc.scalar.copy(out=hres[b][i], in_=back[:])
 
-        def put(b, i):
-            nc.vector.tensor_tensor(page[b][i][:].indirect(list2[:]), hres[b][i], wgsd[i][:], ALU.mult)
+        def put(b, i, js=slice(0, S)):
+            entries = list2[:, js.start // 16 : js.stop // 16]
+            nc.vector.tensor_tensor(page[b][i][:].indirect(entries), hres[b][i][:, js], wgsd[i][:, js], ALU.mult)
 
-        def pick(x, b, i):
-            nc.vector.tensor_tensor(x[:, i, :], page[b][i][:].indirect(list3[:]), wgt_t[:], ALU.mult)
+        def pick(dst, b, i, ms):
+            entries = list3[:, ms.start // 16 : ms.stop // 16]
+            nc.vector.tensor_tensor(dst, page[b][i][:].indirect(entries), wgt_t[:, ms], ALU.mult)
 
         def display(obank, b, hf, codes, scales):
             for q in range(NT // 2):
@@ -211,15 +216,34 @@ def tile_list_cable_tension_display_kernel(
                         stop=(b == HB - 1 and u == 1),
                     )
 
-        nc.vector.tensor_copy(vs[:], tabs[:].indirect(list1[:]))
+        wgs_bank = bank(4, [P, S // P, P])
+        for c in range(S // P):
+            nc.tensor.transpose(wgs_bank[:, c, :], wgs_t[:, c * P : (c + 1) * P], ident[:])
+        nc.scalar.copy(
+            out=wgs_turned[:].rearrange("p c i (r q) -> p c r q i", r=4),
+            in_=wgs_bank[:].rearrange("p c (q i) -> p c q i", i=PACK).unsqueeze(2).to_broadcast([P, S // P, 4, 32, PACK]),
+        )
+        for i in range(PACK):
+            dealt = bank(4 + i, [P, S])
+            for c in range(S // P):
+                nc.tensor.transpose(dealt[:, c * P : (c + 1) * P], wgs_turned[:, c, i, :], ident[:])
+            nc.scalar.copy(out=wgsd[i][:], in_=dealt[:])
+
+        halves = [slice(0, S // 2), slice(S // 2, S)]
         for a in range(KP):
             quantise_w1(0, a, a == KP - 1)
-            nc.vector.tensor_copy(vw[a][:], tabw[a][:].bitcast(U32).indirect(list1[:]))
+            if a == 0:
+                vs = kept([P, S], U8, "w1raw00")
+                nc.vector.tensor_copy(vs[:], tabs[:].indirect(list1[:]))
+            for js in halves if a == KP - 1 else [slice(0, S)]:
+                nc.vector.tensor_copy(vw[a][:, js], tabw[a][:].bitcast(U32).indirect(list1[:, js.start // 16 : js.stop // 16]))
 
-        features(0, 0, True)
-        put(0, 0)
-        for i in range(1, PACK):
-            features(0, i, i == 1)
+        for number, js in enumerate(halves):
+            features_on_vector(0, 0, number, js)
+            put(0, 0, js)
+        features_on_vector(0, 1, 2, slice(0, S))
+        for i in range(2, PACK):
+            features_on_tensor(0, i, (i + 1) % PACK)
         put(0, 1)
         quantise_w1(1, 0, False)
         put(0, 2)
@@ -227,7 +251,7 @@ def tile_list_cable_tension_display_kernel(
         put(0, 3)
         quantise_w1(1, 2, False)
         for i in range(PACK):
-            pick(x, 0, i)
+            pick(x[:, i, :], 0, i, slice(0, M))
         for i in range(PACK):
             nc.vector.tensor_scalar(out=zplanes[:, i, :], in0=x[:, i, :], scalar1=thr_t[:, 0, i : i + 1], scalar2=None, op0=ALU.max)
         nc.scalar.copy(
@@ -235,8 +259,9 @@ def tile_list_cable_tension_display_kernel(
             in_=zplanes[:].rearrange("p t (c i) -> p c t i", i=4),
         )
 
-        for i in range(PACK):
-            features(1, i, False)
+        features_on_vector(1, 0, 1, slice(0, S))
+        for i in range(1, PACK):
+            features_on_tensor(1, i, (i + 1) % PACK)
         put(1, 0)
         nc.vector.quantize_mx(out=z0c[:].bitcast(FP8X4), scales=z0s[:], in_=z0[:])
         obank = [[bank(2 + 3 * hf + q, [P, 2, HALF]) for q in range(NT // 2)] for hf in range(2)]
@@ -244,21 +269,37 @@ def tile_list_cable_tension_display_kernel(
             display(obank, 0, hf, z0c[:, hf * HALF : (hf + 1) * HALF], z0s[:, hf * HALF : (hf + 1) * HALF])
         for i in range(1, PACK):
             put(1, i)
-        x = kept([P, PACK, M], F32, "h1")
-        for i in range(PACK):
-            pick(x, 1, i)
-        floor = thr_t[:, 1, :].unsqueeze(1).unsqueeze(3).to_broadcast([P, HALF // 4, PACK, 4])
-        for hf in range(2):
-            nc.vector.tensor_tensor(
-                z1[hf][:].rearrange("p (c i t) -> p c t i", i=4, t=PACK),
-                x[:, :, hf * HALF : (hf + 1) * HALF].rearrange("p t (c i) -> p c t i", i=4),
-                floor,
-                ALU.max,
+        x1 = kept([P, 2, PACK, HALF], F32, "h1")
+
+        def pick_half(hf):
+            for i in range(PACK):
+                pick(x1[:, hf, i, :], 1, i, slice(hf * HALF, (hf + 1) * HALF))
+
+        def bound_half(hf):
+            planes = kept([P, PACK, HALF], BF16, f"w1raw0{hf}")
+            for i in range(PACK):
+                nc.vector.tensor_scalar(out=planes[:, i, :], in0=x1[:, hf, i, :], scalar1=thr_t[:, 1, i : i + 1], scalar2=None, op0=ALU.max)
+            nc.scalar.copy(
+                out=z1[hf][:].rearrange("p (c i t) -> p c t i", i=4, t=PACK),
+                in_=planes[:].rearrange("p t (c i) -> p c t i", i=4),
             )
-        for hf in range(2):
+
+        def multiply_half(hf):
             nc.vector.quantize_mx(out=z1c[hf][:].bitcast(FP8X4), scales=z1s[hf][:], in_=z1[hf][:])
             display(obank, 1, hf, z1c[hf][:], z1s[hf][:])
-        for hf in range(2):
-            for q in range(NT // 2):
-                nc.vector.tensor_tensor(acc[hf][q][:], obank[hf][q][:], acc[hf][q][:], ALU.add)
-                nc.sync.dma_start(out=out_v[q, :, :, hf * HALF : (hf + 1) * HALF], in_=acc[hf][q][:])
+
+        def finish(hf, q):
+            nc.vector.tensor_tensor(acc[hf][q][:], obank[hf][q][:], acc[hf][q][:], ALU.add)
+            nc.sync.dma_start(out=out_v[q, :, :, hf * HALF : (hf + 1) * HALF], in_=acc[hf][q][:])
+
+        pick_half(0)
+        bound_half(0)
+        multiply_half(0)
+        pick_half(1)
+        bound_half(1)
+        finish(0, 0)
+        finish(0, 1)
+        multiply_half(1)
+        finish(0, 2)
+        for q in range(NT // 2):
+            finish(1, q)

@@ -61,7 +61,6 @@ def tile_list_cable_tension_display_kernel(
         w4s = kept([P, HB, N], U8, "w4s")
         x = kept([P, PACK, M], F32, "x")
         zplanes = kept([P, PACK, M], BF16, "zplanes")
-        z0 = kept([P, M * PACK], BF16, "z0")
         z0c = kept([P, M], U32, "z0c")
         z0s = kept([P, M], U8, "z0s")
         z1 = [kept([P, HALF * PACK], BF16, f"z1{hf}") for hf in range(2)]
@@ -105,13 +104,13 @@ def tile_list_cable_tension_display_kernel(
         nc.sync.dma_start(out=wgs_t[:], in_=wgs)
         load_w1(0, 0)
         load_tab(0)
+        nc.sync.dma_start(list2[:], offs2)
+        nc.scalar.dma_start(out=gain_t[:], in_=gain.rearrange("(b p i) -> p b i", b=HB, i=PACK))
         load_w1(0, 1)
         load_tab(1)
         load_w1(0, 2)
         load_tab(2)
-        nc.sync.dma_start(out=gain_t[:], in_=gain.rearrange("(b p i) -> p b i", b=HB, i=PACK))
         load_res(0, 0)
-        nc.sync.dma_start(list2[:], offs2)
         load_page(0, 0)
         load_res(0, 1)
         load_page(0, 1)
@@ -167,7 +166,7 @@ def tile_list_cable_tension_display_kernel(
                     start=(a == 0),
                     stop=(a == KP - 1),
                 )
-            bounded = ring.tile([P, width], F32, name="bounded", bufs=4)
+            bounded = ring.tile([P, width], F32, name="bounded", bufs=5)
             nc.scalar.activation(out=bounded[:], in_=y[:], func=ACT.Tanh)
             return bounded
 
@@ -186,7 +185,7 @@ def tile_list_cable_tension_display_kernel(
                 block = slice(c * P, (c + 1) * P)
                 nc.tensor.matmul(turned[:, block], hres[b][i][:, block], ident[:], start=True, stop=False, is_transpose=True)
                 nc.tensor.matmul(turned[:, block], scaled[:, block], ident[:], start=False, stop=True, is_transpose=True)
-            summed = ring.tile([P, S], F32, name="summed", bufs=2)
+            summed = ring.tile([P, S], F32, name="summed", bufs=2, align_bytes=64)
             nc.scalar.copy(out=summed[:], in_=turned[:])
             back = bank(6 + i % 2, [P, S])
             for c in range(S // P):
@@ -229,7 +228,7 @@ def tile_list_cable_tension_display_kernel(
                 nc.tensor.transpose(dealt[:, c * P : (c + 1) * P], wgs_turned[:, c, i, :], ident[:])
             nc.scalar.copy(out=wgsd[i][:], in_=dealt[:])
 
-        halves = [slice(0, S // 2), slice(S // 2, S)]
+        halves = [slice(0, S // 4), slice(S // 4, S // 2), slice(S // 2, S)]
         for a in range(KP):
             quantise_w1(0, a, a == KP - 1)
             if a == 0:
@@ -241,9 +240,9 @@ def tile_list_cable_tension_display_kernel(
         for number, js in enumerate(halves):
             features_on_vector(0, 0, number, js)
             put(0, 0, js)
-        features_on_vector(0, 1, 2, slice(0, S))
+        features_on_vector(0, 1, 3, slice(0, S))
         for i in range(2, PACK):
-            features_on_tensor(0, i, (i + 1) % PACK)
+            features_on_tensor(0, i, i - 2)
         put(0, 1)
         quantise_w1(1, 0, False)
         put(0, 2)
@@ -254,15 +253,16 @@ def tile_list_cable_tension_display_kernel(
             pick(x[:, i, :], 0, i, slice(0, M))
         for i in range(PACK):
             nc.vector.tensor_scalar(out=zplanes[:, i, :], in0=x[:, i, :], scalar1=thr_t[:, 0, i : i + 1], scalar2=None, op0=ALU.max)
+
+        features_on_vector(1, 0, 0, slice(0, S))
+        for i in range(1, PACK):
+            features_on_tensor(1, i, i)
+        put(1, 0)
+        z0 = ring.tile([P, M * PACK], BF16, name="summed", bufs=2, align_bytes=64)
         nc.scalar.copy(
             out=z0[:].rearrange("p (c i t) -> p c t i", i=4, t=PACK),
             in_=zplanes[:].rearrange("p t (c i) -> p c t i", i=4),
         )
-
-        features_on_vector(1, 0, 1, slice(0, S))
-        for i in range(1, PACK):
-            features_on_tensor(1, i, (i + 1) % PACK)
-        put(1, 0)
         nc.vector.quantize_mx(out=z0c[:].bitcast(FP8X4), scales=z0s[:], in_=z0[:])
         obank = [[bank(2 + 3 * hf + q, [P, 2, HALF]) for q in range(NT // 2)] for hf in range(2)]
         for hf in range(2):

from contextlib import ExitStack

import concourse.mybir as mybir
from concourse.masks import make_identity

K, T, S, H, T2, M, N = 1536, 2048, 512, 1024, 1024, 512, 768
FLOPS = 2 * K * H * S + 2 * H * N * M

F32 = mybir.dt.float32
BF16 = mybir.dt.bfloat16
I32 = mybir.dt.int32
U32 = mybir.dt.uint32
U16 = mybir.dt.uint16
U8 = mybir.dt.uint8
FP8X4 = mybir.dt.float8_e4m3fn_x4
FP4X4 = mybir.dt.float4_e2m1fn_x4
ALU = mybir.AluOpType
ACT = mybir.ActivationFunctionType

P = 128
PACK = 4
PASS = P * PACK
KP = K // PASS
HB = H // PASS
NT = N // P
HALF = M // 2


def tile_list_cable_tension_display_kernel(
    tc, tab_words, tab_scales, offs, offs2, offs3, w1, gain, res, wgs, page0, wgt, thr, w4_words, w4_scales, base, out
):
    nc = tc.nc
    with ExitStack() as ctx:
        keep = ctx.enter_context(tc.tile_pool(name="keep", bufs=1))
        ring = ctx.enter_context(tc.tile_pool(name="ring", bufs=3))
        psum = ctx.enter_context(tc.psum_pool(name="psum", bufs=1))

        def kept(shape, dtype, name):
            return keep.tile(shape, dtype, name=name, align_bytes=64)

        list1 = kept([P, S // 16], U16, "list1")
        list2 = kept([P, S // 16], U16, "list2")
        list3 = kept([P, M // 16], U16, "list3")
        tabw = [kept([P, T], I32, f"tabw{a}") for a in range(KP)]
        tabs = kept([P, T], U8, "tabs")
        vw = [kept([P, S], U32, f"vw{a}") for a in range(KP)]
        w1raw = [[kept([P, PACK, PASS], F32, f"w1raw{b}{a}") for a in range(KP)] for b in range(HB)]
        w1c = [[kept([P, PASS], U32, f"w1c{b}{a}") for a in range(KP)] for b in range(HB)]
        w1s = [[kept([P, PASS], U8, f"w1s{b}{a}") for a in range(KP)] for b in range(HB)]
        page = [[kept([P, T2], F32, f"page{b}{i}") for i in range(PACK)] for b in range(HB)]
        h0 = [kept([P, S], F32, f"h0{i}") for i in range(PACK)]
        h1 = kept([P, PACK, S], F32, "h1")
        hres = [[t[:] for t in h0], [h1[:, i, :] for i in range(PACK)]]
        wgsd = [kept([P, S], F32, f"wgsd{i}") for i in range(PACK)]
        wgs_t = kept([P, S], F32, "wgs_t")
        wgs_turned = kept([P, S // P, PACK, P], F32, "wgs_turned")
        wgt_t = kept([P, M], F32, "wgt_t")
        gain_t = kept([P, HB, PACK], F32, "gain_t")
        thr_t = kept([P, HB, PACK], F32, "thr_t")
        w4w = kept([P, HB, 2 * N], U8, "w4w")
        w4s = kept([P, HB, N], U8, "w4s")
        x = kept([P, PACK, M], F32, "x")
        zplanes = kept([P, PACK, M], BF16, "zplanes")
        z0c = kept([P, M], U32, "z0c")
        z0s = kept([P, M], U8, "z0s")
        z1 = [kept([P, HALF * PACK], BF16, f"z1{hf}") for hf in range(2)]
        z1c = [kept([P, HALF], U32, f"z1c{hf}") for hf in range(2)]
        z1s = [kept([P, HALF], U8, f"z1s{hf}") for hf in range(2)]
        acc = [[kept([P, 2, HALF], F32, f"acc{hf}{q}") for q in range(NT // 2)] for hf in range(2)]
        ident = kept([P, P], F32, "ident")

        def bank(number, shape):
            return psum.tile(shape, F32, name=f"bank{number}")

        res_v = res.rearrange("(b p i) j -> b i p j", b=HB, i=PACK)
        page_v = page0.rearrange("(b p i) c -> b i p c", b=HB, i=PACK)
        base_v = base.rearrange("(q u p) m -> q p u m", u=2, p=P)
        out_v = out.rearrange("(q u p) m -> q p u m", u=2, p=P)

        def load_w1(b, a):
            rows = w1[a * PASS : (a + 1) * PASS, b * PASS : (b + 1) * PASS]
            nc.sync.dma_start(out=w1raw[b][a][:], in_=rows.rearrange("(p j) c -> p j c", j=PACK))

        def load_tab(a):
            nc.sync.dma_start(out=tabw[a][:], in_=tab_words[a].rearrange("p n t -> p (n t)").bitcast(I32))

        def load_res(b, i):
            nc.sync.dma_start(out=hres[b][i], in_=res_v[b, i])

        def load_page(b, i):
            nc.sync.dma_start(out=page[b][i][:], in_=page_v[b, i])

        nc.gpsimd.memset(tabs[:].bitcast(I32), 0)
        make_identity(nc, ident[:])
        for quad in range(4):
            nc.gpsimd.dma_start(
                out=tabs[32 * quad : 32 * quad + PACK * KP, :].bitcast(I32),
                in_=tab_scales[:, PACK * quad : PACK * (quad + 1), :].bitcast(I32),
            )

        nc.gpsimd.memset(w4s[:].bitcast(I32), 0)

        nc.sync.dma_start(list1[:], offs)
        nc.sync.dma_start(out=wgs_t[:], in_=wgs)
        load_w1(0, 0)
        load_tab(0)
        nc.sync.dma_start(list2[:], offs2)
        nc.scalar.dma_start(out=gain_t[:], in_=gain.rearrange("(b p i) -> p b i", b=HB, i=PACK))
        load_w1(0, 1)
        load_tab(1)
        load_w1(0, 2)
        load_tab(2)
        load_res(0, 0)
        load_page(0, 0)
        load_res(0, 1)
        load_page(0, 1)
        load_res(0, 2)
        load_res(0, 3)
        load_w1(1, 0)
        load_page(0, 2)
        load_w1(1, 1)
        load_page(0, 3)
        load_w1(1, 2)
        load_res(1, 0)
        load_res(1, 1)
        nc.sync.dma_start(list3[:], offs3)
        nc.sync.dma_start(out=thr_t[:], in_=thr.rearrange("(b p i) -> p b i", b=HB, i=PACK))
        nc.sync.dma_start(out=wgt_t[:], in_=wgt)
        load_res(1, 2)
        load_res(1, 3)
        for i in range(PACK):
            load_page(1, i)
        for quad in range(4):
            nc.sync.dma_start(
                out=w4s[32 * quad : 32 * quad + PACK, :, :].bitcast(I32),
                in_=w4_scales[:, PACK * quad : PACK * (quad + 1), :].rearrange("a r n -> r a n").bitcast(I32),
            )
        nc.sync.dma_start(out=w4w[:].bitcast(I32), in_=w4_words.rearrange("a p n -> p a n").bitcast(I32))
        for hf in range(2):
            for q in range(NT // 2):
                nc.sync.dma_start(out=acc[hf][q][:], in_=base_v[q, :, :, hf * HALF : (hf + 1) * HALF])

        def quantise_w1(b, a, on_vector):
            grouped = ring.tile([P, PASS * PACK], BF16, name="grouped", align_bytes=64)
            dst = grouped[:].rearrange("p (t m j) -> p m j t", t=PACK, j=PACK)
            src = w1raw[b][a][:].rearrange("p j (m t) -> p m j t", t=PACK)
            if on_vector:
                nc.vector.tensor_copy(out=dst, in_=src)
            else:
                for part in range(2):
                    cut = slice(part * P // 2, (part + 1) * P // 2)
                    nc.scalar.copy(out=dst[:, cut], in_=src[:, cut])
            nc.vector.quantize_mx(out=w1c[b][a][:].bitcast(FP8X4), scales=w1s[b][a][:], in_=grouped[:])

        def bounded_response(b, i, number, js):
            width = js.stop - js.start
            y = bank(number, [P, width])
            cols = slice(i * P, (i + 1) * P)
            for a in range(KP):
                nc.tensor.matmul_mx(
                    out=y[:],
                    lhsT=w1c[b][a][:, cols].bitcast(FP8X4),
                    lhsT_scale=w1s[b][a][:, cols],
                    rhs=vw[a][:, js].bitcast(FP8X4),
                    rhs_scale=vs[PACK * a : P, js],
                    start=(a == 0),
                    stop=(a == KP - 1),
                )
            bounded = ring.tile([P, width], F32, name="bounded", bufs=5)
            nc.scalar.activation(out=bounded[:], in_=y[:], func=ACT.Tanh)
            return bounded

        def features_on_vector(b, i, number, js):
            bounded = bounded_response(b, i, number, js)
            nc.vector.scalar_tensor_tensor(
                out=hres[b][i][:, js], in0=bounded[:], scalar=gain_t[:, b, i : i + 1], in1=hres[b][i][:, js], op0=ALU.mult, op1=ALU.add
            )

        def features_on_tensor(b, i, number):
            bounded = bounded_response(b, i, number, slice(0, S))
            scaled = ring.tile([P, S], F32, name="scaled", bufs=2)
            nc.scalar.activation(out=scaled[:], in_=bounded[:], func=ACT.Copy, scale=gain_t[:, b, i : i + 1])
            turned = bank(4 + i % 2, [P, S])
            for c in range(S // P):
                block = slice(c * P, (c + 1) * P)
                nc.tensor.matmul(turned[:, block], hres[b][i][:, block], ident[:], start=True, stop=False, is_transpose=True)
                nc.tensor.matmul(turned[:, block], scaled[:, block], ident[:], start=False, stop=True, is_transpose=True)
            summed = ring.tile([P, S], F32, name="summed", bufs=2, align_bytes=64)
            nc.scalar.copy(out=summed[:], in_=turned[:])
            back = bank(6 + i % 2, [P, S])
            for c in range(S // P):
                block = slice(c * P, (c + 1) * P)
                nc.tensor.transpose(back[:, block], summed[:, block], ident[:])
            nc.scalar.copy(out=hres[b][i], in_=back[:])

        def put(b, i, js=slice(0, S)):
            entries = list2[:, js.start // 16 : js.stop // 16]
            nc.vector.tensor_tensor(page[b][i][:].indirect(entries), hres[b][i][:, js], wgsd[i][:, js], ALU.mult)

        def pick(dst, b, i, ms):
            entries = list3[:, ms.start // 16 : ms.stop // 16]
            nc.vector.tensor_tensor(dst, page[b][i][:].indirect(entries), wgt_t[:, ms], ALU.mult)

        def display(obank, b, hf, codes, scales):
            for q in range(NT // 2):
                for u in range(2):
                    n = 2 * q + u
                    nc.tensor.matmul_mx(
                        out=obank[hf][q][:, u, :],
                        lhsT=w4w[:, b, 2 * P * n : 2 * P * (n + 1)].bitcast(FP4X4),
                        lhsT_scale=w4s[:, b, P * n : P * (n + 1)],
                        rhs=codes.bitcast(FP8X4),
                        rhs_scale=scales,
                        start=(b == 0 and u == 0),
                        stop=(b == HB - 1 and u == 1),
                    )

        wgs_bank = bank(4, [P, S // P, P])
        for c in range(S // P):
            nc.tensor.transpose(wgs_bank[:, c, :], wgs_t[:, c * P : (c + 1) * P], ident[:])
        nc.scalar.copy(
            out=wgs_turned[:].rearrange("p c i (r q) -> p c r q i", r=4),
            in_=wgs_bank[:].rearrange("p c (q i) -> p c q i", i=PACK).unsqueeze(2).to_broadcast([P, S // P, 4, 32, PACK]),
        )
        for i in range(PACK):
            dealt = bank(4 + i, [P, S])
            for c in range(S // P):
                nc.tensor.transpose(dealt[:, c * P : (c + 1) * P], wgs_turned[:, c, i, :], ident[:])
            nc.scalar.copy(out=wgsd[i][:], in_=dealt[:])

        halves = [slice(0, S // 4), slice(S // 4, S // 2), slice(S // 2, S)]
        for a in range(KP):
            quantise_w1(0, a, a == KP - 1)
            if a == 0:
                vs = kept([P, S], U8, "w1raw00")
                nc.vector.tensor_copy(vs[:], tabs[:].indirect(list1[:]))
            for js in halves if a == KP - 1 else [slice(0, S)]:
                nc.vector.tensor_copy(vw[a][:, js], tabw[a][:].bitcast(U32).indirect(list1[:, js.start // 16 : js.stop // 16]))

        for number, js in enumerate(halves):
            features_on_vector(0, 0, number, js)
            put(0, 0, js)
        features_on_vector(0, 1, 3, slice(0, S))
        for i in range(2, PACK):
            features_on_tensor(0, i, i - 2)
        put(0, 1)
        quantise_w1(1, 0, False)
        put(0, 2)
        quantise_w1(1, 1, False)
        put(0, 3)
        quantise_w1(1, 2, False)
        for i in range(PACK):
            pick(x[:, i, :], 0, i, slice(0, M))
        for i in range(PACK):
            nc.vector.tensor_scalar(out=zplanes[:, i, :], in0=x[:, i, :], scalar1=thr_t[:, 0, i : i + 1], scalar2=None, op0=ALU.max)

        features_on_vector(1, 0, 0, slice(0, S))
        for i in range(1, PACK):
            features_on_tensor(1, i, i)
        put(1, 0)
        z0 = ring.tile([P, M * PACK], BF16, name="summed", bufs=2, align_bytes=64)
        nc.scalar.copy(
            out=z0[:].rearrange("p (c i t) -> p c t i", i=4, t=PACK),
            in_=zplanes[:].rearrange("p t (c i) -> p c t i", i=4),
        )
        nc.vector.quantize_mx(out=z0c[:].bitcast(FP8X4), scales=z0s[:], in_=z0[:])
        obank = [[bank(2 + 3 * hf + q, [P, 2, HALF]) for q in range(NT // 2)] for hf in range(2)]
        for hf in range(2):
            display(obank, 0, hf, z0c[:, hf * HALF : (hf + 1) * HALF], z0s[:, hf * HALF : (hf + 1) * HALF])
        for i in range(1, PACK):
            put(1, i)
        x1 = kept([P, 2, PACK, HALF], F32, "h1")

        def pick_half(hf):
            for i in range(PACK):
                pick(x1[:, hf, i, :], 1, i, slice(hf * HALF, (hf + 1) * HALF))

        def bound_half(hf):
            planes = kept([P, PACK, HALF], BF16, f"w1raw0{hf}")
            for i in range(PACK):
                nc.vector.tensor_scalar(out=planes[:, i, :], in0=x1[:, hf, i, :], scalar1=thr_t[:, 1, i : i + 1], scalar2=None, op0=ALU.max)
            nc.scalar.copy(
                out=z1[hf][:].rearrange("p (c i t) -> p c t i", i=4, t=PACK),
                in_=planes[:].rearrange("p t (c i) -> p c t i", i=4),
            )

        def multiply_half(hf):
            nc.vector.quantize_mx(out=z1c[hf][:].bitcast(FP8X4), scales=z1s[hf][:], in_=z1[hf][:])
            display(obank, 1, hf, z1c[hf][:], z1s[hf][:])

        def finish(hf, q):
            nc.vector.tensor_tensor(acc[hf][q][:], obank[hf][q][:], acc[hf][q][:], ALU.add)
            nc.sync.dma_start(out=out_v[q, :, :, hf * HALF : (hf + 1) * HALF], in_=acc[hf][q][:])

        pick_half(0)
        bound_half(0)
        multiply_half(0)
        pick_half(1)
        bound_half(1)
        finish(0, 0)
        finish(0, 1)
        multiply_half(1)
        finish(0, 2)
        for q in range(NT // 2):
            finish(1, q)
